import numpy as np
import ml_dtypes


def mxq(x, axis, fmt="e4m3"):
    dtype, down = {"e4m3": (ml_dtypes.float8_e4m3fn, 7), "e5m2": (ml_dtypes.float8_e5m2, 14)}[fmt]
    v = np.moveaxis(np.asarray(x, np.float32).astype(ml_dtypes.bfloat16).astype(np.float64), axis, -1)
    blocks = v.reshape(v.shape[:-1] + (-1, 32))
    amax = np.abs(blocks).max(-1, keepdims=True)
    byte = np.maximum(np.where(amax > 0, np.frexp(amax)[1] - 1 + 127, 0) - down, 1)
    scale = np.exp2(byte - 127.0)
    codes = (blocks / scale).astype(np.float32).astype(dtype).astype(np.float64)
    return np.moveaxis((codes * scale).reshape(v.shape), -1, axis)


WIDE = False


def mx_kscale(k):
    if not WIDE:
        return np.ones(k)
    levels = np.array([10, -10, 5, -5, 0])
    if k % 512:
        return np.exp2(np.random.permutation(np.resize(levels, k // 32))).repeat(32)
    a = np.empty((k // 512, 16))
    for p in range(k // 512):
        a[p, :8] = np.random.permutation(np.resize(levels, 8))
        for g in range(8):
            far = levels[np.abs(levels - a[p, g]) >= 10]
            a[p, g + 8] = far[np.random.randint(len(far))]
    return np.exp2(a.ravel()).repeat(32)


def f64(x):
    return np.asarray(x).astype(np.float64)


def striped(idx):
    return np.tile(idx.reshape(-1, 16).T, (8, 1)).astype(np.uint16)


def unstriped(offs):
    return offs[:16].T.reshape(-1).astype(np.int64)


def striped8(idx):
    return np.concatenate([x.reshape(-1, 16).T for x in idx]).astype(np.uint16)


def runs(offs, k):
    lists = np.stack([offs[16 * r : 16 * r + 16].T.reshape(-1) for r in range(8)]).astype(np.int64)
    return lists[np.arange(k) % 512 // 64]


def pack_weight(w):
    k, n = w.shape
    w = f64(np.asarray(w, np.float32).astype(ml_dtypes.bfloat16)).reshape(k // 32, 32, n)
    amax = np.abs(w).max(1)
    byte = np.clip(np.where(amax > 0, np.frexp(amax)[1] - 1 + 127 - 7, 1), 1, 254)
    scaled = (w * np.exp2(127.0 - byte)[:, None, :]).reshape(k, n).astype(np.float32)
    words = np.ascontiguousarray(scaled.reshape(k // 512, 128, 4, n).transpose(0, 1, 3, 2)).astype(ml_dtypes.float8_e4m3fn).view(np.uint8)
    return words, np.ascontiguousarray(byte.astype(np.uint8).reshape(k // 512, 16, n))


def unpack_weight(words, scales):
    g, p, n, _ = words.shape
    vals = np.ascontiguousarray(words).view(ml_dtypes.float8_e4m3fn).astype(np.float64) * np.repeat(np.exp2(scales.astype(np.float64) - 127.0), 8, axis=1)[..., None]
    return vals.transpose(0, 1, 3, 2).reshape(g * 512, n)


def sigmoid(v):
    return 1.0 / (1.0 + np.exp(-np.maximum(v, -700.0)))


K, T, S, N, H, C = 512, 2048, 512, 512, 512, 512


def setup_inputs():
    n = np.random.standard_normal
    s = mx_kscale(K)[:, None]
    u = mx_kscale(S)
    packed_xT = pack_weight(n((K, T)) * s)
    return {
        "x_words": packed_xT[0],
        "x_scales": packed_xT[1],
        "w1": (n((K, H)) / np.sqrt(K) / s).astype(np.float32),
        "w2": (n((K, H)) / np.sqrt(K) / s).astype(np.float32),
        "gn": (np.random.uniform(0.5, 1.5, (H, 1)) * u[:, None]).astype(np.float32),
        "w3": (n((H, N)) / np.sqrt(H) / u[:, None]).astype(np.float32),
        "gs": (np.random.uniform(0.5, 1.5, (K, 1)) / s).astype(np.float32),
        "offs": striped(np.random.permutation(T)[:S]),
        "two": striped(np.random.permutation(T)[:S]),
        "n1": striped8(np.stack([np.random.permutation(S) for _ in range(8)])),
        "n2": striped8(np.stack([np.random.permutation(S) for _ in range(8)])),
        "n3": striped8(np.stack([np.random.permutation(S) for _ in range(8)])),
        "n4": striped8(np.stack([np.random.permutation(S) for _ in range(8)])),
        "cand": striped(np.random.permutation(T)[:C]),
        "n5": striped8(np.stack([np.random.permutation(S) for _ in range(8)])),
        "n6": striped8(np.stack([np.random.permutation(S) for _ in range(8)])),
    }


def reference(x_words, x_scales, w1, w2, gn, w3, gs, offs, two, n1, n2, n3, n4, cand, n5, n6):
    xq = unpack_weight(x_words, x_scales)[:, unstriped(offs)]
    y = mxq(f64(w1), 0, "e4m3").T @ xq
    st = y * (sigmoid(y[np.arange(H)[:, None], runs(n1, H)]))
    z = f64(gn) * (st - (st[np.arange(H)[:, None], runs(n2, H)]))
    a = mxq(f64(w3), 0, "e4m3").T @ mxq(z, 0, "e4m3")
    x_cand = unpack_weight(x_words, x_scales)[:, unstriped(cand)]
    x_two = unpack_weight(x_words, x_scales)[:, unstriped(two)]
    d = mxq(f64(w2), 0, "e4m3").T @ x_two
    pa = d[np.arange(H)[:, None], runs(n3, H)]
    kr = np.exp(-0.5 * ((d - pa) ** 2))
    pb = d[np.arange(H)[:, None], runs(n4, H)]
    kr2 = np.exp(-0.5 * ((d - pb) ** 2))
    z2 = f64(gs) * ((kr * pa + kr2 * pb) / (kr + kr2 + 0.5))
    b = 0.0625 * ((x_cand.T @ mxq(z2, 0, "e4m3")))
    return (a + a[np.arange(N)[:, None], runs(n5, N)]) * (sigmoid(b + b[np.arange(C)[:, None], runs(n6, C)]))

@@ -1,0 +1,240 @@
+from contextlib import ExitStack
+
+import concourse.mybir as mybir
+
+K, T, S = 512, 2048, 512
+FLOPS = 4 * 2 * 512 * 512 * 512
+
+F32 = mybir.dt.float32
+BF16 = mybir.dt.bfloat16
+I32 = mybir.dt.int32
+U32 = mybir.dt.uint32
+U16 = mybir.dt.uint16
+U8 = mybir.dt.uint8
+FP8X4 = mybir.dt.float8_e4m3fn_x4
+ACT = mybir.ActivationFunctionType
+ALU = mybir.AluOpType
+
+P = 128
+PACK = 4
+HALF = S // 2
+HALVES = [(slice(h * HALF, (h + 1) * HALF), slice(h * HALF // 16, (h + 1) * HALF // 16)) for h in range(2)]
+
+
+def tile_picked_tfcdtriebhopgkern_none_p_kernel(
+    tc, x_words, x_scales, w1, w2, gn, w3, gs, offs, two, n1, n2, n3, n4, cand, n5, n6, out
+):
+    nc = tc.nc
+    with ExitStack() as ctx:
+        keep = ctx.enter_context(tc.tile_pool(name="keep", bufs=1))
+        psum = ctx.enter_context(tc.psum_pool(name="psum", bufs=1))
+
+        def planes(name):
+            return [keep.tile([P, S], F32, name=f"{name}{t}") for t in range(PACK)]
+
+        def load_list(src, name):
+            tile = keep.tile([P, S // 16], U16, name=name)
+            nc.sync.dma_start(tile[:], src)
+            return tile
+
+        def load_weight(w, name):
+            halves = []
+            for h in range(2):
+                raw = keep.tile([P, PACK, HALF], F32, name=f"{name}_raw{h}")
+                nc.sync.dma_start(out=raw[:], in_=w[:, h * HALF : (h + 1) * HALF].rearrange("(p j) c -> p j c", j=PACK))
+                halves.append(raw)
+            return halves
+
+        def load_gain(g, name):
+            tile = keep.tile([P, PACK], F32, name=name)
+            nc.sync.dma_start(out=tile[:], in_=g.rearrange("(p t) o -> p (t o)", t=PACK))
+            return tile
+
+        def round_weight(halves, name, copy):
+            grouped = keep.tile([P, PACK * S], BF16, name=f"{name}_bf", align_bytes=64)
+            dealt = grouped[:].rearrange("p (t m j) -> p m j t", t=PACK, j=PACK)
+            for h, raw in enumerate(halves):
+                ms = slice(h * HALF // PACK, (h + 1) * HALF // PACK)
+                copy(out=dealt[:, ms], in_=raw[:].rearrange("p j (m t) -> p m j t", t=PACK))
+            return grouped
+
+        def copy_scalar(out, in_):
+            nc.scalar.activation(out=out, in_=in_, func=ACT.Copy)
+
+        def mx_tiles(name):
+            words = keep.tile([P, S], U32, name=f"{name}_words", align_bytes=64)
+            scales = keep.tile([P, S], U8, name=f"{name}_scales", align_bytes=64)
+            return words, scales
+
+        def quantize(values, operand, cols):
+            words, scales = operand
+            nc.vector.quantize_mx(out=words[:, cols].bitcast(FP8X4), scales=scales[:, cols], in_=values)
+
+        def product(stationary, moving, t, bank):
+            acc = psum.tile([P, S], F32, name="acc", tag=f"bank{bank}")
+            cols = slice(t * P, (t + 1) * P)
+            nc.tensor.matmul_mx(
+                out=acc[:],
+                lhsT=stationary[0][:, cols].bitcast(FP8X4),
+                lhsT_scale=stationary[1][:, cols],
+                rhs=moving[0][:].bitcast(FP8X4),
+                rhs_scale=moving[1][:],
+                start=True,
+                stop=True,
+            )
+            return acc
+
+        def fetch_scalar(dst, window, places, scale=1.0, bias=0.0):
+            for cols, lcols in HALVES:
+                nc.scalar.activation(out=dst[:, cols], in_=window[:].indirect(places[:, lcols]), func=ACT.Copy, scale=scale, bias=bias)
+
+        def fetch_vector(dst, window, places):
+            for cols, lcols in HALVES:
+                nc.vector.tensor_copy(out=dst[:, cols], in_=window[:].indirect(places[:, lcols]))
+
+        def fetch_fused(dst, window, places, other, op):
+            for cols, lcols in HALVES:
+                nc.vector.tensor_tensor(out=dst[:, cols], in0=window[:].indirect(places[:, lcols]), in1=other[:, cols], op=op)
+
+        x_rows = keep.tile([P, T // PACK], I32, name="x_rows")
+        for q in range(4):
+            nc.sync.dma_start(out=x_rows[32 * q : 32 * q + 4, :], in_=x_scales[0, 4 * q : 4 * q + 4, :].bitcast(I32))
+        two_l = load_list(two, "two_l")
+        w2_raw = load_weight(w2, "w2")
+        x_tab = keep.tile([P, T], I32, name="x_tab")
+        nc.sync.dma_start(out=x_tab[:], in_=x_words[0].rearrange("p n t -> p (n t)").bitcast(I32))
+        offs_l = load_list(offs, "offs_l")
+        cand_l = load_list(cand, "cand_l")
+        n3_l = load_list(n3, "n3_l")
+        n4_l = load_list(n4, "n4_l")
+        w1_raw = load_weight(w1, "w1")
+        gs_t = load_gain(gs, "gs_t")
+        gn_t = load_gain(gn, "gn_t")
+        n1_l = load_list(n1, "n1_l")
+        n2_l = load_list(n2, "n2_l")
+        w3_raw = load_weight(w3, "w3")
+        n5_l = load_list(n5, "n5_l")
+        n6_l = load_list(n6, "n6_l")
+        x_bytes = keep.tile([P, T], U8, name="x_bytes")
+        nc.vector.memset(x_bytes[:].bitcast(I32), 0)
+        for q in range(4):
+            nc.vector.tensor_copy(out=x_bytes[32 * q : 32 * q + 4, :].bitcast(I32), in_=x_rows[32 * q : 32 * q + 4, :])
+
+        def pick_words(operand, places, dealt):
+            dst = operand[0][:].rearrange("p (t m) -> p m t", t=PACK) if dealt else operand[0][:]
+            nc.vector.tensor_copy(out=dst, in_=x_tab[:].bitcast(U32).indirect(places[:]))
+
+        def pick_bytes(operand, places, dealt):
+            dst = operand[1][:].rearrange("p (t m) -> p m t", t=PACK) if dealt else operand[1][:]
+            nc.vector.tensor_copy(out=dst, in_=x_bytes[:].indirect(places[:]))
+
+        x_two, x_offs, x_cand = mx_tiles("x_two"), mx_tiles("x_offs"), mx_tiles("x_cand")
+        w1_q, w2_q, w3_q = mx_tiles("w1"), mx_tiles("w2"), mx_tiles("w3")
+        z_q, z2_q = mx_tiles("z"), mx_tiles("z2")
+        whole = slice(0, S)
+
+        quantize(round_weight(w2_raw, "w2", copy_scalar)[:], w2_q, whole)
+        pick_words(x_two, two_l, False)
+        pick_bytes(x_two, two_l, False)
+        pick_bytes(x_offs, offs_l, False)
+        pick_words(x_offs, offs_l, False)
+        quantize(round_weight(w1_raw, "w1", nc.vector.tensor_copy)[:], w1_q, whole)
+        d_win, pa, pb, ka, kb = planes("d"), planes("pa"), planes("pb"), planes("ka"), planes("kb")
+        for t in range(PACK):
+            acc = product(w2_q, x_two, t, t)
+            nc.scalar.copy(out=d_win[t][:], in_=acc[:])
+            fetch_scalar(pa[t], d_win[t], n3_l)
+            (fetch_vector if t < 2 else fetch_scalar)(pb[t], d_win[t], n4_l)
+            nc.vector.tensor_tensor(out=ka[t][:], in0=pa[t][:], in1=d_win[t][:], op=ALU.subtract)
+            nc.vector.tensor_tensor(out=kb[t][:], in0=pb[t][:], in1=d_win[t][:], op=ALU.subtract)
+
+        th_win, sg, st_win, st_twin = planes("th"), planes("sg"), planes("st"), planes("st_twin")
+        y_acc = []
+        for t in range(PACK):
+            y_acc.append(product(w1_q, x_offs, t, PACK + t))
+            nc.scalar.activation(out=th_win[t][:], in_=y_acc[t][:], func=ACT.Tanh, scale=0.5)
+
+        num = keep.tile([P, PACK, S], F32, name="num")
+        den = keep.tile([P, PACK, S], F32, name="den")
+        z_f = keep.tile([P, PACK, S], F32, name="z_f")
+        a_win, a_twin, a_sum = planes("a"), planes("a_twin"), planes("a_sum")
+        b_win, gate = planes("b"), planes("gate")
+        for t in range(PACK):
+            fetch_scalar(sg[t], th_win[t], n1_l, scale=0.5, bias=0.5)
+            nc.vector.scalar_tensor_tensor(
+                out=st_win[t][:], in0=y_acc[t][:], scalar=gn_t[:, t : t + 1], in1=sg[t][:], op0=ALU.mult, op1=ALU.mult
+            )
+            nc.sync.dma_start(out=st_twin[t][:], in_=st_win[t][:])
+
+
+        quantize(round_weight(w3_raw, "w3", nc.vector.tensor_copy)[:], w3_q, whole)
+
+        for t in range(PACK):
+            fetch_fused(z_f[:, t, :], st_win[t], n2_l, st_twin[t], ALU.subtract)
+        z_bf = keep.tile([P, S * PACK], BF16, name="z_bf", align_bytes=64)
+        nc.vector.tensor_scalar(
+            out=z_bf[:].rearrange("p (c i t) -> p c t i", i=4, t=PACK),
+            in0=z_f[:].rearrange("p t (c i) -> p c t i", i=4),
+            scalar1=-1.0,
+            scalar2=None,
+            op0=ALU.mult,
+        )
+        quantize(z_bf[:], z_q, whole)
+
+        for t in range(PACK):
+            for k in (ka, kb):
+                nc.scalar.activation(out=k[t][:], in_=k[t][:], func=ACT.Square)
+            for k in (ka, kb):
+                nc.scalar.activation(out=k[t][:], in_=k[t][:], func=ACT.Exp, scale=-0.5)
+            nc.vector.scalar_tensor_tensor(
+                out=den[:, t, :], in0=ka[t][:], scalar=0.5, in1=kb[t][:], op0=ALU.add, op1=ALU.add
+            )
+            if t in [3]:
+                nc.vector.tensor_tensor(out=den[:, t, :], in0=den[:, t, :], in1=den[:, t, :], op=ALU.mult)
+            else:
+                nc.scalar.activation(out=den[:, t, :], in_=den[:, t, :], func=ACT.Square)
+            for k, p_ in ((ka, pa), (kb, pb)):
+                nc.vector.scalar_tensor_tensor(
+                    out=p_[t][:], in0=k[t][:], scalar=gs_t[:, t : t + 1], in1=p_[t][:], op0=ALU.mult, op1=ALU.mult
+                )
+            nc.vector.tensor_tensor(out=num[:, t, :], in0=pa[t][:], in1=pb[t][:], op=ALU.add)
+
+        pick_bytes(x_cand, cand_l, True)
+        pick_words(x_cand, cand_l, True)
+
+        for jb in range(PACK):
+            cols = slice(jb * P, (jb + 1) * P)
+            rec = keep.tile([P, PACK, P], F32, name=f"rec{jb}")
+            nc.scalar.activation(out=rec[:], in_=den[:, :, cols], func=ACT.Abs_reciprocal_sqrt)
+            z2_bf = keep.tile([P, P * PACK], BF16, name=f"z2_bf{jb}", align_bytes=64)
+            nc.vector.tensor_tensor(
+                out=z2_bf[:].rearrange("p (c i t) -> p c t i", i=4, t=PACK),
+                in0=num[:, :, cols].rearrange("p t (c i) -> p c t i", i=4),
+                in1=rec[:].rearrange("p t (c i) -> p c t i", i=4),
+                op=ALU.mult,
+            )
+            quantize(z2_bf[:], z2_q, cols)
+
+
+        for t in range(PACK):
+            acc = product(w3_q, z_q, t, t)
+            nc.scalar.activation(out=a_win[t][:], in_=acc[:], func=ACT.Copy, scale=0.5)
+            nc.sync.dma_start(out=a_twin[t][:], in_=a_win[t][:])
+
+        for t in range(PACK):
+            fetch_fused(a_sum[t], a_win[t], n5_l, a_twin[t], ALU.add)
+
+        out_rows = out.rearrange("(p t) n -> t p n", t=PACK)
+        b_acc = []
+        for t in range(PACK):
+            b_acc.append(product(x_cand, z2_q, t, PACK + t))
+            nc.scalar.copy(out=b_win[t][:], in_=b_acc[t][:])
+        for t in range(PACK):
+            (fetch_vector if t in [0,1] else fetch_scalar)(gate[t], b_win[t], n6_l)
+            for cols in [whole]:
+                nc.vector.tensor_tensor(out=gate[t][:, cols], in0=gate[t][:, cols], in1=b_acc[t][:, cols], op=ALU.add)
+                nc.scalar.activation(out=gate[t][:, cols], in_=gate[t][:, cols], func=ACT.Tanh, scale=0.03125)
+                nc.vector.scalar_tensor_tensor(
+                    out=gate[t][:, cols], in0=gate[t][:, cols], scalar=1.0, in1=a_sum[t][:, cols], op0=ALU.add, op1=ALU.mult
+                )
+                nc.sync.dma_start(out=out_rows[t][:, cols], in_=gate[t][:, cols])

@@ -1,8 +1,10 @@
 from contextlib import ExitStack
 
 import concourse.mybir as mybir
+from concourse.masks import make_identity
 
 K, T, S = 512, 2048, 512
+O = {"pe_u":[0,1,2,3],"pe_d":[],"tbanks":[4,5,6,7],"dbanks":[0,1,0,1],"ybanks":[2,3,2,3],"abanks":[0,1,0,1],"bbanks":[2,3,0,1],"w1":"V","w3":"V","zc":"V","dc":"SSSS","ac":"SSSS","bc":"SSSS","n1":"SSSV","n2":"SSSS","n3":"SSSV","n4":"VVVV","n5":"SVSV","n6":"SSVV","sqa":"SSSS","sqb":"SSSS","dsq":"VSSS","num":"VVVV","order":[["xt",0],["w2",0],["xo",0],["w1",0],["d",0],["pa",0],["pb",0],["d",1],["pa",1],["pb",1],["d",2],["pa",2],["pb",2],["d",3],["pa",3],["pb",3],["y",0],["st",0],["sq",0],["ex",0],["y",1],["st",1],["sq",1],["ex",1],["y",2],["st",2],["sq",2],["ex",2],["y",3],["st",3],["sq",3],["ex",3],["w3",0],["zf",0],["den",0],["pr",0],["zf",1],["den",1],["pr",1],["zf",2],["den",2],["pr",2],["zf",3],["den",3],["pr",3],["zq",0],["xc",0],["j",0],["j",1],["j",2],["j",3],["am",0],["am",1],["am",2],["am",3],["bm",0],["bm",1],["bm",2],["bm",3],["as",0],["g",0],["o",0],["as",1],["g",1],["o",1],["as",2],["g",2],["o",2],["as",3],["g",3],["o",3]],"loads":"two w2 x offs cand n3 n4 w1 gs gn n1 n2 w3 n5 n6","cand_tag":"x_offs","w2":"S","zh":1,"mode":"M","vbanks":[],"stage":1}
 FLOPS = 4 * 2 * 512 * 512 * 512
 
 F32 = mybir.dt.float32
@@ -92,32 +94,47 @@ def tile_picked_tfcdtriebhopgkern_none_p_kernel(
             for cols, lcols in HALVES:
                 nc.vector.tensor_copy(out=dst[:, cols], in_=window[:].indirect(places[:, lcols]))
 
+        def fetch_vector_negated(dst, window, places):
+            for cols, lcols in HALVES:
+                nc.vector.tensor_scalar(
+                    out=dst[:, cols], in0=window[:].indirect(places[:, lcols]), scalar1=-1.0, scalar2=0.0, op0=ALU.mult, op1=ALU.add
+                )
+
+        def fetch_scalar_negated(dst, window, places):
+            fetch_scalar(dst, window, places, scale=-1.0)
+
+        nturn = {}
+        def turn(*tiles, pool='tbanks'):
+            nturn[pool] = nturn.get(pool, 0) + 1
+            acc = psum.tile([P, S], F32, name="turned", tag=f"bank{O[pool][nturn[pool] % len(O[pool])]}")
+            for jb in range(PACK):
+                cols = slice(jb * P, (jb + 1) * P)
+                for n, tile in enumerate(tiles):
+                    nc.tensor.matmul(
+                        out=acc[:, cols], lhsT=tile[:, cols], rhs=ident[:], start=n == 0, stop=n == len(tiles) - 1, is_transpose=True
+                    )
+            return acc
+
         def fetch_fused(dst, window, places, other, op):
             for cols, lcols in HALVES:
                 nc.vector.tensor_tensor(out=dst[:, cols], in0=window[:].indirect(places[:, lcols]), in1=other[:, cols], op=op)
 
-        x_rows = keep.tile([P, T // PACK], I32, name="x_rows")
-        for q in range(4):
-            nc.sync.dma_start(out=x_rows[32 * q : 32 * q + 4, :], in_=x_scales[0, 4 * q : 4 * q + 4, :].bitcast(I32))
-        two_l = load_list(two, "two_l")
-        w2_raw = load_weight(w2, "w2")
-        x_tab = keep.tile([P, T], I32, name="x_tab")
-        nc.sync.dma_start(out=x_tab[:], in_=x_words[0].rearrange("p n t -> p (n t)").bitcast(I32))
-        offs_l = load_list(offs, "offs_l")
-        cand_l = load_list(cand, "cand_l")
-        n3_l = load_list(n3, "n3_l")
-        n4_l = load_list(n4, "n4_l")
-        w1_raw = load_weight(w1, "w1")
-        gs_t = load_gain(gs, "gs_t")
-        gn_t = load_gain(gn, "gn_t")
-        n1_l = load_list(n1, "n1_l")
-        n2_l = load_list(n2, "n2_l")
-        w3_raw = load_weight(w3, "w3")
-        n5_l = load_list(n5, "n5_l")
-        n6_l = load_list(n6, "n6_l")
         x_bytes = keep.tile([P, T], U8, name="x_bytes")
         nc.vector.memset(x_bytes[:].bitcast(I32), 0)
+        x_rows = keep.tile([P, T // PACK], I32, name="x_rows") if O['stage'] else x_bytes[:].bitcast(I32)
         for q in range(4):
+            (nc.sync if O['stage'] else nc.scalar).dma_start(out=x_rows[32 * q : 32 * q + 4, :], in_=x_scales[0, 4 * q : 4 * q + 4, :].bitcast(I32))
+        LD = {}
+        src = dict(two=two, offs=offs, cand=cand, n1=n1, n2=n2, n3=n3, n4=n4, n5=n5, n6=n6, w1=w1, w2=w2, w3=w3, gs=gs, gn=gn)
+        for nm in O['loads'].split():
+            if nm == 'x':
+                x_tab = keep.tile([P, T], I32, name="x_tab")
+                nc.sync.dma_start(out=x_tab[:], in_=x_words[0].rearrange("p n t -> p (n t)").bitcast(I32))
+            elif nm[0] == 'w': LD[nm] = load_weight(src[nm], nm)
+            elif nm[0] == 'g': LD[nm] = load_gain(src[nm], nm)
+            else: LD[nm] = load_list(src[nm], nm)
+        two_l, offs_l, cand_l, n1_l, n2_l, n3_l, n4_l, n5_l, n6_l, w1_raw, w2_raw, w3_raw, gs_t, gn_t = [LD[k] for k in src]
+        for q in range(4 if O['stage'] else 0):
             nc.vector.tensor_copy(out=x_bytes[32 * q : 32 * q + 4, :].bitcast(I32), in_=x_rows[32 * q : 32 * q + 4, :])
 
         def pick_words(operand, places, dealt):
@@ -128,81 +145,122 @@ def tile_picked_tfcdtriebhopgkern_none_p_kernel(
             dst = operand[1][:].rearrange("p (t m) -> p m t", t=PACK) if dealt else operand[1][:]
             nc.vector.tensor_copy(out=dst, in_=x_bytes[:].indirect(places[:]))
 
-        x_two, x_offs, x_cand = mx_tiles("x_two"), mx_tiles("x_offs"), mx_tiles("x_cand")
+        x_two, x_offs = mx_tiles("x_two"), mx_tiles("x_offs")
+        late = {}
         w1_q, w2_q, w3_q = mx_tiles("w1"), mx_tiles("w2"), mx_tiles("w3")
         z_q, z2_q = mx_tiles("z"), mx_tiles("z2")
         whole = slice(0, S)
 
-        quantize(round_weight(w2_raw, "w2", copy_scalar)[:], w2_q, whole)
-        pick_words(x_two, two_l, False)
-        pick_bytes(x_two, two_l, False)
-        pick_bytes(x_offs, offs_l, False)
-        pick_words(x_offs, offs_l, False)
-        quantize(round_weight(w1_raw, "w1", nc.vector.tensor_copy)[:], w1_q, whole)
+
+        ident = keep.tile([P, P], F32, name="ident")
+        if O['pe_u'] or O['pe_d']:
+            make_identity(nc, ident[:])
+        half_t = None
         d_win, pa, pb, ka, kb = planes("d"), planes("pa"), planes("pb"), planes("ka"), planes("kb")
-        for t in range(PACK):
-            acc = product(w2_q, x_two, t, t)
-            nc.scalar.copy(out=d_win[t][:], in_=acc[:])
-            fetch_scalar(pa[t], d_win[t], n3_l)
-            (fetch_vector if t < 2 else fetch_scalar)(pb[t], d_win[t], n4_l)
-            nc.vector.tensor_tensor(out=ka[t][:], in0=pa[t][:], in1=d_win[t][:], op=ALU.subtract)
-            nc.vector.tensor_tensor(out=kb[t][:], in0=pb[t][:], in1=d_win[t][:], op=ALU.subtract)
-
-        th_win, sg, st_win, st_twin = planes("th"), planes("sg"), planes("st"), planes("st_twin")
-        y_acc = []
-        for t in range(PACK):
-            y_acc.append(product(w1_q, x_offs, t, PACK + t))
-            nc.scalar.activation(out=th_win[t][:], in_=y_acc[t][:], func=ACT.Tanh, scale=0.5)
-
+        th_win, sg, st_win, st_twin = planes("th"), planes("sg"), planes("st"), None
         num = keep.tile([P, PACK, S], F32, name="num")
         den = keep.tile([P, PACK, S], F32, name="den")
         z_f = keep.tile([P, PACK, S], F32, name="z_f")
         a_win, a_twin, a_sum = planes("a"), planes("a_twin"), planes("a_sum")
         b_win, gate = planes("b"), planes("gate")
-        for t in range(PACK):
-            fetch_scalar(sg[t], th_win[t], n1_l, scale=0.5, bias=0.5)
-            nc.vector.scalar_tensor_tensor(
-                out=st_win[t][:], in0=y_acc[t][:], scalar=gn_t[:, t : t + 1], in1=sg[t][:], op0=ALU.mult, op1=ALU.mult
-            )
-            nc.sync.dma_start(out=st_twin[t][:], in_=st_win[t][:])
-
-
-        quantize(round_weight(w3_raw, "w3", nc.vector.tensor_copy)[:], w3_q, whole)
-
-        for t in range(PACK):
-            fetch_fused(z_f[:, t, :], st_win[t], n2_l, st_twin[t], ALU.subtract)
+        st4 = keep.tile([P, PACK, S], F32, name="st4")
+        y_acc, b_acc, a_acc, us = {}, {}, {}, {}
+        out_rows = out.rearrange("(p t) n -> t p n", t=PACK)
         z_bf = keep.tile([P, S * PACK], BF16, name="z_bf", align_bytes=64)
-        nc.vector.tensor_scalar(
-            out=z_bf[:].rearrange("p (c i t) -> p c t i", i=4, t=PACK),
-            in0=z_f[:].rearrange("p t (c i) -> p c t i", i=4),
-            scalar1=-1.0,
-            scalar2=None,
-            op0=ALU.mult,
-        )
-        quantize(z_bf[:], z_q, whole)
-
-        for t in range(PACK):
-            for k in (ka, kb):
-                nc.scalar.activation(out=k[t][:], in_=k[t][:], func=ACT.Square)
-            for k in (ka, kb):
-                nc.scalar.activation(out=k[t][:], in_=k[t][:], func=ACT.Exp, scale=-0.5)
-            nc.vector.scalar_tensor_tensor(
-                out=den[:, t, :], in0=ka[t][:], scalar=0.5, in1=kb[t][:], op0=ALU.add, op1=ALU.add
-            )
-            if t in [3]:
-                nc.vector.tensor_tensor(out=den[:, t, :], in0=den[:, t, :], in1=den[:, t, :], op=ALU.mult)
+        V, Sc, G = nc.vector, nc.scalar, nc.gpsimd
+        def cp(e): return {'V': V.tensor_copy, 'S': copy_scalar, 'G': G.tensor_copy}[e]
+        def evac(e, out, in_, scale=1.0):
+            if e == 'S': Sc.activation(out=out, in_=in_, func=ACT.Copy, scale=scale)
+            elif scale == 1.0: V.tensor_copy(out=out, in_=in_)
+            else: V.tensor_scalar(out=out, in0=in_, scalar1=scale, scalar2=None, op0=ALU.mult)
+        def fetch(e, dst, window, places, scale=1.0, bias=0.0):
+            if e == 'S':
+                fetch_scalar(dst, window, places, scale=scale, bias=bias)
+            elif scale == 1.0:
+                fetch_vector(dst, window, places)
             else:
-                nc.scalar.activation(out=den[:, t, :], in_=den[:, t, :], func=ACT.Square)
+                for cols, lcols in HALVES:
+                    V.tensor_scalar(out=dst[:, cols], in0=window[:].indirect(places[:, lcols]), scalar1=scale, scalar2=bias, op0=ALU.mult, op1=ALU.add)
+        def tt(e, o, a, b, op=ALU.add): (G if e == 'G' else V).tensor_tensor(out=o, in0=a, in1=b, op=op)
+        def stt(o, a, s, b, op0, op1): V.scalar_tensor_tensor(out=o, in0=a, scalar=s, in1=b, op0=op0, op1=op1)
+        gs_neg = keep.tile([P, PACK], F32, name="gs_neg")
+        if O['pe_u']:
+            V.tensor_scalar(out=gs_neg[:], in0=gs_t[:], scalar1=-1.0, scalar2=None, op0=ALU.mult)
+        def sq(e, o, a):
+            if e == 'S': Sc.activation(out=o, in_=a, func=ACT.Square)
+            else: tt(e, o, a, a, ALU.mult)
+        def s_w2(t):
+            quantize(round_weight(w2_raw, "w2", cp(O['w2']))[:], w2_q, whole)
+        def s_xt(t):
+            pick_words(x_two, two_l, False)
+            pick_bytes(x_two, two_l, False)
+        def s_xo(t):
+            pick_bytes(x_offs, offs_l, False)
+            pick_words(x_offs, offs_l, False)
+        def s_xc(t):
+            late['cand'] = mx_tiles(O['cand_tag'])
+            pick_bytes(late['cand'], cand_l, True)
+            pick_words(late['cand'], cand_l, True)
+        def s_w1(t): quantize(round_weight(w1_raw, "w1", cp(O['w1']))[:], w1_q, whole)
+        def s_w3(t): quantize(round_weight(w3_raw, "w3", cp(O['w3']))[:], w3_q, whole)
+        def s_d(t):
+            acc = product(w2_q, x_two, t, O['dbanks'][t])
+            evac(O['dc'][t], d_win[t][:], acc[:])
+        def s_pa(t):
+            fetch(O['n3'][t], pa[t], d_win[t], n3_l, -1.0 if t in O['pe_u'] else 1.0)
+            if t not in O['pe_u']: tt('V', ka[t][:], pa[t][:], d_win[t][:], ALU.subtract)
+        def s_pb(t):
+            fetch(O['n4'][t], pb[t], d_win[t], n4_l, -1.0 if t in O['pe_u'] else 1.0)
+            if t not in O['pe_u']: tt('V', kb[t][:], pb[t][:], d_win[t][:], ALU.subtract)
+        def s_sq(t):
+            if t in O['pe_u']:
+                ua, ub = turn(d_win[t], pa[t]), turn(d_win[t], pb[t])
+                sq('S', ka[t][:], ua[:]); sq('S', kb[t][:], ub[:])
+            else:
+                sq(O['sqa'][t], ka[t][:], ka[t][:]); sq(O['sqb'][t], kb[t][:], kb[t][:])
+        def s_ex(t):
+            for k in (ka, kb):
+                src = turn(k[t]) if (t in O['pe_u'] and O['mode'] == 'M') else k[t]
+                Sc.activation(out=k[t][:], in_=src[:], func=ACT.Exp, scale=-0.5)
+        def s_den(t):
+            if t in O['pe_u'] and O['mode'] == 'Y':
+                both = turn(ka[t], kb[t])
+                Sc.activation(out=den[:, t, :], in_=both[:], func=ACT.Square, bias=half_t[:])
+            else:
+                stt(den[:, t, :], ka[t][:], 0.5, kb[t][:], ALU.add, ALU.add)
+                sq(O['dsq'][t], den[:, t, :], den[:, t, :])
+        def s_pr(t):
             for k, p_ in ((ka, pa), (kb, pb)):
-                nc.vector.scalar_tensor_tensor(
-                    out=p_[t][:], in0=k[t][:], scalar=gs_t[:, t : t + 1], in1=p_[t][:], op0=ALU.mult, op1=ALU.mult
-                )
-            nc.vector.tensor_tensor(out=num[:, t, :], in0=pa[t][:], in1=pb[t][:], op=ALU.add)
-
-        pick_bytes(x_cand, cand_l, True)
-        pick_words(x_cand, cand_l, True)
-
-        for jb in range(PACK):
+                back = turn(k[t], pool='vbanks') if (t in O['pe_u'] and O['mode'] == 'Y') else k[t]
+                stt(p_[t][:], back[:], (gs_neg if t in O['pe_u'] else gs_t)[:, t : t + 1], p_[t][:], ALU.mult, ALU.mult)
+            tt(O['num'][t], num[:, t, :], pa[t][:], pb[t][:])
+        def s_y(t):
+            y_acc[t] = product(w1_q, x_offs, t, O['ybanks'][t])
+            Sc.activation(out=th_win[t][:], in_=y_acc[t][:], func=ACT.Tanh, scale=0.5)
+        def s_st(t):
+            fetch(O['n1'][t], sg[t], th_win[t], n1_l, 0.5, 0.5)
+            stt(st_win[t][:], y_acc[t][:], gn_t[:, t : t + 1], sg[t][:], ALU.mult, ALU.mult)
+            nc.sync.dma_start(out=st4[:, t, :], in_=st_win[t][:])
+        def s_zf(t):
+            if O['n2'] == 'FFFF': fetch_fused(z_f[:, t, :], st_win[t], n2_l, st4[:, t, :], ALU.subtract)
+            else: fetch(O['n2'][t], z_f[:, t, :], st_win[t], n2_l)
+        def s_zq(t):
+            for h in range(O['zh']):
+                w = S // O['zh']
+                cols = slice(h * w, (h + 1) * w)
+                if O['n2'] == 'FFFF': V.tensor_scalar(out=z_bf[:, h * w * 4:(h + 1) * w * 4].rearrange("p (c i t) -> p c t i", i=4, t=PACK), in0=z_f[:, :, cols].rearrange("p t (c i) -> p c t i", i=4), scalar1=-1.0, scalar2=None, op0=ALU.mult)
+                else: V.tensor_tensor(out=z_bf[:, h * w * 4:(h + 1) * w * 4].rearrange("p (c i t) -> p c t i", i=4, t=PACK), in0=st4[:, :, cols].rearrange("p t (c i) -> p c t i", i=4), in1=z_f[:, :, cols].rearrange("p t (c i) -> p c t i", i=4), op=ALU.subtract)
+                quantize(z_bf[:, h * w * 4:(h + 1) * w * 4], z_q, cols)
+        def s_am(t):
+            a_acc[t] = product(w3_q, z_q, t, O['abanks'][t])
+            evac(O['ac'][t], a_win[t][:], a_acc[t][:], 0.5)
+            if O['n5'][t] == 'F': nc.sync.dma_start(out=a_twin[t][:], in_=a_win[t][:])
+        def s_as(t):
+            if O['n5'][t] == 'F': fetch_fused(a_sum[t], a_win[t], n5_l, a_twin[t], ALU.add)
+            else:
+                fetch(O['n5'][t], a_twin[t], a_win[t], n5_l)
+                tt('V', a_sum[t][:], a_win[t][:], a_twin[t][:])
+        def s_j(jb):
             cols = slice(jb * P, (jb + 1) * P)
             rec = keep.tile([P, PACK, P], F32, name=f"rec{jb}")
             nc.scalar.activation(out=rec[:], in_=den[:, :, cols], func=ACT.Abs_reciprocal_sqrt)
@@ -214,27 +272,17 @@ def tile_picked_tfcdtriebhopgkern_none_p_kernel(
                 op=ALU.mult,
             )
             quantize(z2_bf[:], z2_q, cols)
-
-
-        for t in range(PACK):
-            acc = product(w3_q, z_q, t, t)
-            nc.scalar.activation(out=a_win[t][:], in_=acc[:], func=ACT.Copy, scale=0.5)
-            nc.sync.dma_start(out=a_twin[t][:], in_=a_win[t][:])
-
-        for t in range(PACK):
-            fetch_fused(a_sum[t], a_win[t], n5_l, a_twin[t], ALU.add)
-
-        out_rows = out.rearrange("(p t) n -> t p n", t=PACK)
-        b_acc = []
-        for t in range(PACK):
-            b_acc.append(product(x_cand, z2_q, t, PACK + t))
-            nc.scalar.copy(out=b_win[t][:], in_=b_acc[t][:])
-        for t in range(PACK):
-            (fetch_vector if t in [0,1] else fetch_scalar)(gate[t], b_win[t], n6_l)
-            for cols in [whole]:
-                nc.vector.tensor_tensor(out=gate[t][:, cols], in0=gate[t][:, cols], in1=b_acc[t][:, cols], op=ALU.add)
-                nc.scalar.activation(out=gate[t][:, cols], in_=gate[t][:, cols], func=ACT.Tanh, scale=0.03125)
-                nc.vector.scalar_tensor_tensor(
-                    out=gate[t][:, cols], in0=gate[t][:, cols], scalar=1.0, in1=a_sum[t][:, cols], op0=ALU.add, op1=ALU.mult
-                )
-                nc.sync.dma_start(out=out_rows[t][:, cols], in_=gate[t][:, cols])
+        def s_bm(t):
+            b_acc[t] = product(late['cand'], z2_q, t, O['bbanks'][t])
+            evac(O['bc'][t], b_win[t][:], b_acc[t][:])
+        def s_g(t):
+            fetch(O['n6'][t], gate[t], b_win[t], n6_l)
+            tt('V', gate[t][:], gate[t][:], b_acc[t][:])
+            nc.scalar.activation(out=gate[t][:], in_=gate[t][:], func=ACT.Tanh, scale=0.03125)
+        def s_o(t):
+            stt(gate[t][:], gate[t][:], 1.0, a_sum[t][:], ALU.add, ALU.mult)
+            nc.sync.dma_start(out=out_rows[t], in_=gate[t][:])
+        L = dict(w1=s_w1, w2=s_w2, w3=s_w3, xt=s_xt, xo=s_xo, xc=s_xc, d=s_d, pa=s_pa, pb=s_pb, sq=s_sq, ex=s_ex, den=s_den, pr=s_pr, y=s_y, st=s_st, zf=s_zf, zq=s_zq, am=s_am, j=s_j, bm=s_bm, g=s_g, o=s_o)
+        L['as'] = s_as
+        for name, t in O['order']:
+            L[name](t)

@@ -3,8 +3,7 @@ from contextlib import ExitStack
 import concourse.mybir as mybir
 from concourse.masks import make_identity
 
-K, T, S = 512, 2048, 512
-O = {"pe_u":[0,1,2,3],"pe_d":[],"tbanks":[4,5,6,7],"dbanks":[0,1,0,1],"ybanks":[2,3,2,3],"abanks":[0,1,0,1],"bbanks":[2,3,0,1],"w1":"V","w3":"V","zc":"V","dc":"SSSS","ac":"SSSS","bc":"SSSS","n1":"SSSV","n2":"SSSS","n3":"SSSV","n4":"VVVV","n5":"SVSV","n6":"SSVV","sqa":"SSSS","sqb":"SSSS","dsq":"VSSS","num":"VVVV","order":[["xt",0],["w2",0],["xo",0],["w1",0],["d",0],["pa",0],["pb",0],["d",1],["pa",1],["pb",1],["d",2],["pa",2],["pb",2],["d",3],["pa",3],["pb",3],["y",0],["st",0],["sq",0],["ex",0],["y",1],["st",1],["sq",1],["ex",1],["y",2],["st",2],["sq",2],["ex",2],["y",3],["st",3],["sq",3],["ex",3],["w3",0],["zf",0],["den",0],["pr",0],["zf",1],["den",1],["pr",1],["zf",2],["den",2],["pr",2],["zf",3],["den",3],["pr",3],["zq",0],["xc",0],["j",0],["j",1],["j",2],["j",3],["am",0],["am",1],["am",2],["am",3],["bm",0],["bm",1],["bm",2],["bm",3],["as",0],["g",0],["o",0],["as",1],["g",1],["o",1],["as",2],["g",2],["o",2],["as",3],["g",3],["o",3]],"loads":"two w2 x offs cand n3 n4 w1 gs gn n1 n2 w3 n5 n6","cand_tag":"x_offs","w2":"S","zh":1,"mode":"M","vbanks":[],"stage":1}
+T, S = 2048, 512
 FLOPS = 4 * 2 * 512 * 512 * 512
 
 F32 = mybir.dt.float32
@@ -19,8 +18,21 @@ ALU = mybir.AluOpType
 
 P = 128
 PACK = 4
+PLANES = range(PACK)
+QUADRANT = 32
+LIST_ROWS = 16
+LINE = 4
+ALL = slice(0, S)
 HALF = S // 2
-HALVES = [(slice(h * HALF, (h + 1) * HALF), slice(h * HALF // 16, (h + 1) * HALF // 16)) for h in range(2)]
+HALVES = [(slice(h * HALF, (h + 1) * HALF), slice(h * HALF // LIST_ROWS, (h + 1) * HALF // LIST_ROWS)) for h in range(2)]
+
+DA_BANKS, Y_BANKS, B_BANKS, TURN_BANKS = (0, 1), (2, 3), (2, 3, 0, 1), (4, 5, 6, 7)
+
+VECTOR_N1_N3 = (3,)
+VECTOR_N6 = (1, 3)
+VECTOR_B_COPY = (0, 1)
+VECTOR_DEN_SQUARE = (0,)
+SCALAR_N5 = (0,)
 
 
 def tile_picked_tfcdtriebhopgkern_none_p_kernel(
@@ -32,36 +44,30 @@ def tile_picked_tfcdtriebhopgkern_none_p_kernel(
         psum = ctx.enter_context(tc.psum_pool(name="psum", bufs=1))
 
         def planes(name):
-            return [keep.tile([P, S], F32, name=f"{name}{t}") for t in range(PACK)]
+            return [keep.tile([P, S], F32, name=f"{name}{t}") for t in PLANES]
+
+        def joined_planes(name):
+            return keep.tile([P, PACK, S], F32, name=name)
 
         def load_list(src, name):
-            tile = keep.tile([P, S // 16], U16, name=name)
+            tile = keep.tile([P, S // LIST_ROWS], U16, name=name)
             nc.sync.dma_start(tile[:], src)
             return tile
 
-        def load_weight(w, name):
-            halves = []
-            for h in range(2):
-                raw = keep.tile([P, PACK, HALF], F32, name=f"{name}_raw{h}")
-                nc.sync.dma_start(out=raw[:], in_=w[:, h * HALF : (h + 1) * HALF].rearrange("(p j) c -> p j c", j=PACK))
-                halves.append(raw)
-            return halves
+        def load_weight(w, name, pieces):
+            rows = w.rearrange("(p j) c -> p j c", j=PACK)
+            step = PACK // pieces
+            raws = []
+            for h in range(pieces):
+                raw = keep.tile([P, step, S], F32, name=f"{name}_raw{h}")
+                nc.sync.dma_start(out=raw[:], in_=rows[:, h * step : (h + 1) * step, :])
+                raws.append(raw)
+            return raws
 
         def load_gain(g, name):
             tile = keep.tile([P, PACK], F32, name=name)
             nc.sync.dma_start(out=tile[:], in_=g.rearrange("(p t) o -> p (t o)", t=PACK))
             return tile
-
-        def round_weight(halves, name, copy):
-            grouped = keep.tile([P, PACK * S], BF16, name=f"{name}_bf", align_bytes=64)
-            dealt = grouped[:].rearrange("p (t m j) -> p m j t", t=PACK, j=PACK)
-            for h, raw in enumerate(halves):
-                ms = slice(h * HALF // PACK, (h + 1) * HALF // PACK)
-                copy(out=dealt[:, ms], in_=raw[:].rearrange("p j (m t) -> p m j t", t=PACK))
-            return grouped
-
-        def copy_scalar(out, in_):
-            nc.scalar.activation(out=out, in_=in_, func=ACT.Copy)
 
         def mx_tiles(name):
             words = keep.tile([P, S], U32, name=f"{name}_words", align_bytes=64)
@@ -71,6 +77,19 @@ def tile_picked_tfcdtriebhopgkern_none_p_kernel(
         def quantize(values, operand, cols):
             words, scales = operand
             nc.vector.quantize_mx(out=words[:, cols].bitcast(FP8X4), scales=scales[:, cols], in_=values)
+
+        def copy_on_scalar(out, in_, scale=1.0):
+            nc.scalar.activation(out=out, in_=in_, func=ACT.Copy, scale=scale)
+
+        def quantize_weight(raws, name, copy):
+            grouped = keep.tile([P, PACK * S], BF16, name=f"{name}_bf", align_bytes=64)
+            dealt = grouped[:].rearrange("p (t m j) -> p m j t", t=PACK, j=PACK)
+            step = PACK // len(raws)
+            for h, raw in enumerate(raws):
+                copy(out=dealt[:, :, h * step : (h + 1) * step, :], in_=raw[:].rearrange("p j (m t) -> p m j t", t=PACK))
+            operand = mx_tiles(name)
+            quantize(grouped[:], operand, ALL)
+            return operand
 
         def product(stationary, moving, t, bank):
             acc = psum.tile([P, S], F32, name="acc", tag=f"bank{bank}")
@@ -86,203 +105,182 @@ def tile_picked_tfcdtriebhopgkern_none_p_kernel(
             )
             return acc
 
-        def fetch_scalar(dst, window, places, scale=1.0, bias=0.0):
-            for cols, lcols in HALVES:
-                nc.scalar.activation(out=dst[:, cols], in_=window[:].indirect(places[:, lcols]), func=ACT.Copy, scale=scale, bias=bias)
+        turns = []
 
-        def fetch_vector(dst, window, places):
-            for cols, lcols in HALVES:
-                nc.vector.tensor_copy(out=dst[:, cols], in_=window[:].indirect(places[:, lcols]))
-
-        def fetch_vector_negated(dst, window, places):
-            for cols, lcols in HALVES:
-                nc.vector.tensor_scalar(
-                    out=dst[:, cols], in0=window[:].indirect(places[:, lcols]), scalar1=-1.0, scalar2=0.0, op0=ALU.mult, op1=ALU.add
-                )
-
-        def fetch_scalar_negated(dst, window, places):
-            fetch_scalar(dst, window, places, scale=-1.0)
-
-        nturn = {}
-        def turn(*tiles, pool='tbanks'):
-            nturn[pool] = nturn.get(pool, 0) + 1
-            acc = psum.tile([P, S], F32, name="turned", tag=f"bank{O[pool][nturn[pool] % len(O[pool])]}")
-            for jb in range(PACK):
-                cols = slice(jb * P, (jb + 1) * P)
+        def turn(*tiles):
+            turns.append(tiles)
+            acc = psum.tile([P, S], F32, name="turned", tag=f"bank{TURN_BANKS[len(turns) % len(TURN_BANKS)]}")
+            for block in range(S // P):
+                cols = slice(block * P, (block + 1) * P)
                 for n, tile in enumerate(tiles):
                     nc.tensor.matmul(
-                        out=acc[:, cols], lhsT=tile[:, cols], rhs=ident[:], start=n == 0, stop=n == len(tiles) - 1, is_transpose=True
+                        out=acc[:, cols],
+                        lhsT=tile[:, cols],
+                        rhs=identity[:],
+                        start=n == 0,
+                        stop=n == len(tiles) - 1,
+                        is_transpose=True,
                     )
             return acc
 
-        def fetch_fused(dst, window, places, other, op):
-            for cols, lcols in HALVES:
-                nc.vector.tensor_tensor(out=dst[:, cols], in0=window[:].indirect(places[:, lcols]), in1=other[:, cols], op=op)
+        def fetch(on_vector, dst, window, places):
+            for cols, list_cols in HALVES:
+                picked = window[:].indirect(places[:, list_cols])
+                if on_vector:
+                    nc.vector.tensor_copy(out=dst[:, cols], in_=picked)
+                else:
+                    nc.scalar.activation(out=dst[:, cols], in_=picked, func=ACT.Copy)
+
+        def fetch_affine(on_vector, dst, window, places, scale, bias):
+            for cols, list_cols in HALVES:
+                picked = window[:].indirect(places[:, list_cols])
+                if on_vector:
+                    nc.vector.tensor_scalar(
+                        out=dst[:, cols], in0=picked, scalar1=scale, scalar2=bias, op0=ALU.mult, op1=ALU.add
+                    )
+                else:
+                    nc.scalar.activation(out=dst[:, cols], in_=picked, func=ACT.Copy, scale=scale, bias=bias)
+
+        def interleave(dst, in0, in1, op):
+            nc.vector.tensor_tensor(
+                out=dst.rearrange("p (c i t) -> p c t i", i=LINE, t=PACK),
+                in0=in0.rearrange("p t (c i) -> p c t i", i=LINE),
+                in1=in1.rearrange("p t (c i) -> p c t i", i=LINE),
+                op=op,
+            )
+
+        def scaled(dst, in0, scalar, op0, in1, op1):
+            nc.vector.scalar_tensor_tensor(out=dst, in0=in0, scalar=scalar, in1=in1, op0=op0, op1=op1)
 
         x_bytes = keep.tile([P, T], U8, name="x_bytes")
         nc.vector.memset(x_bytes[:].bitcast(I32), 0)
-        x_rows = keep.tile([P, T // PACK], I32, name="x_rows") if O['stage'] else x_bytes[:].bitcast(I32)
-        for q in range(4):
-            (nc.sync if O['stage'] else nc.scalar).dma_start(out=x_rows[32 * q : 32 * q + 4, :], in_=x_scales[0, 4 * q : 4 * q + 4, :].bitcast(I32))
-        LD = {}
-        src = dict(two=two, offs=offs, cand=cand, n1=n1, n2=n2, n3=n3, n4=n4, n5=n5, n6=n6, w1=w1, w2=w2, w3=w3, gs=gs, gn=gn)
-        for nm in O['loads'].split():
-            if nm == 'x':
-                x_tab = keep.tile([P, T], I32, name="x_tab")
-                nc.sync.dma_start(out=x_tab[:], in_=x_words[0].rearrange("p n t -> p (n t)").bitcast(I32))
-            elif nm[0] == 'w': LD[nm] = load_weight(src[nm], nm)
-            elif nm[0] == 'g': LD[nm] = load_gain(src[nm], nm)
-            else: LD[nm] = load_list(src[nm], nm)
-        two_l, offs_l, cand_l, n1_l, n2_l, n3_l, n4_l, n5_l, n6_l, w1_raw, w2_raw, w3_raw, gs_t, gn_t = [LD[k] for k in src]
-        for q in range(4 if O['stage'] else 0):
-            nc.vector.tensor_copy(out=x_bytes[32 * q : 32 * q + 4, :].bitcast(I32), in_=x_rows[32 * q : 32 * q + 4, :])
+        x_rows = keep.tile([P, T // 4], I32, name="x_rows")
+        scale_rows = [slice(QUADRANT * q, QUADRANT * q + 4) for q in range(P // QUADRANT)]
+        for q, rows in enumerate(scale_rows):
+            nc.sync.dma_start(out=x_rows[rows, :], in_=x_scales[0, 4 * q : 4 * q + 4, :].bitcast(I32))
+        two_l = load_list(two, "two")
+        offs_l = load_list(offs, "offs")
+        w2_raw = load_weight(w2, "w2", pieces=2)
+        x_table = keep.tile([P, T], I32, name="x_table")
+        nc.sync.dma_start(out=x_table[:], in_=x_words[0].rearrange("p n t -> p (n t)").bitcast(I32))
+        n3_l = load_list(n3, "n3")
+        n4_l = load_list(n4, "n4")
+        w1_raw = load_weight(w1, "w1", pieces=1)
+        gs_t = load_gain(gs, "gs")
+        gn_t = load_gain(gn, "gn")
+        n1_l = load_list(n1, "n1")
+        n2_l = load_list(n2, "n2")
+        cand_l = load_list(cand, "cand")
+        w3_raw = load_weight(w3, "w3", pieces=1)
+        n5_l = load_list(n5, "n5")
+        n6_l = load_list(n6, "n6")
+        for rows in scale_rows:
+            nc.vector.tensor_copy(out=x_bytes[rows, :].bitcast(I32), in_=x_rows[rows, :])
 
-        def pick_words(operand, places, dealt):
-            dst = operand[0][:].rearrange("p (t m) -> p m t", t=PACK) if dealt else operand[0][:]
-            nc.vector.tensor_copy(out=dst, in_=x_tab[:].bitcast(U32).indirect(places[:]))
+        def pick_words(dst, places):
+            nc.vector.tensor_copy(out=dst, in_=x_table[:].bitcast(U32).indirect(places[:]))
 
-        def pick_bytes(operand, places, dealt):
-            dst = operand[1][:].rearrange("p (t m) -> p m t", t=PACK) if dealt else operand[1][:]
+        def pick_bytes(dst, places):
             nc.vector.tensor_copy(out=dst, in_=x_bytes[:].indirect(places[:]))
 
-        x_two, x_offs = mx_tiles("x_two"), mx_tiles("x_offs")
-        late = {}
-        w1_q, w2_q, w3_q = mx_tiles("w1"), mx_tiles("w2"), mx_tiles("w3")
-        z_q, z2_q = mx_tiles("z"), mx_tiles("z2")
-        whole = slice(0, S)
-
-
-        ident = keep.tile([P, P], F32, name="ident")
-        if O['pe_u'] or O['pe_d']:
-            make_identity(nc, ident[:])
-        half_t = None
-        d_win, pa, pb, ka, kb = planes("d"), planes("pa"), planes("pb"), planes("ka"), planes("kb")
-        th_win, sg, st_win, st_twin = planes("th"), planes("sg"), planes("st"), None
-        num = keep.tile([P, PACK, S], F32, name="num")
-        den = keep.tile([P, PACK, S], F32, name="den")
-        z_f = keep.tile([P, PACK, S], F32, name="z_f")
-        a_win, a_twin, a_sum = planes("a"), planes("a_twin"), planes("a_sum")
-        b_win, gate = planes("b"), planes("gate")
-        st4 = keep.tile([P, PACK, S], F32, name="st4")
-        y_acc, b_acc, a_acc, us = {}, {}, {}, {}
-        out_rows = out.rearrange("(p t) n -> t p n", t=PACK)
-        z_bf = keep.tile([P, S * PACK], BF16, name="z_bf", align_bytes=64)
-        V, Sc, G = nc.vector, nc.scalar, nc.gpsimd
-        def cp(e): return {'V': V.tensor_copy, 'S': copy_scalar, 'G': G.tensor_copy}[e]
-        def evac(e, out, in_, scale=1.0):
-            if e == 'S': Sc.activation(out=out, in_=in_, func=ACT.Copy, scale=scale)
-            elif scale == 1.0: V.tensor_copy(out=out, in_=in_)
-            else: V.tensor_scalar(out=out, in0=in_, scalar1=scale, scalar2=None, op0=ALU.mult)
-        def fetch(e, dst, window, places, scale=1.0, bias=0.0):
-            if e == 'S':
-                fetch_scalar(dst, window, places, scale=scale, bias=bias)
-            elif scale == 1.0:
-                fetch_vector(dst, window, places)
-            else:
-                for cols, lcols in HALVES:
-                    V.tensor_scalar(out=dst[:, cols], in0=window[:].indirect(places[:, lcols]), scalar1=scale, scalar2=bias, op0=ALU.mult, op1=ALU.add)
-        def tt(e, o, a, b, op=ALU.add): (G if e == 'G' else V).tensor_tensor(out=o, in0=a, in1=b, op=op)
-        def stt(o, a, s, b, op0, op1): V.scalar_tensor_tensor(out=o, in0=a, scalar=s, in1=b, op0=op0, op1=op1)
+        identity = keep.tile([P, P], F32, name="identity")
+        make_identity(nc, identity[:])
         gs_neg = keep.tile([P, PACK], F32, name="gs_neg")
-        if O['pe_u']:
-            V.tensor_scalar(out=gs_neg[:], in0=gs_t[:], scalar1=-1.0, scalar2=None, op0=ALU.mult)
-        def sq(e, o, a):
-            if e == 'S': Sc.activation(out=o, in_=a, func=ACT.Square)
-            else: tt(e, o, a, a, ALU.mult)
-        def s_w2(t):
-            quantize(round_weight(w2_raw, "w2", cp(O['w2']))[:], w2_q, whole)
-        def s_xt(t):
-            pick_words(x_two, two_l, False)
-            pick_bytes(x_two, two_l, False)
-        def s_xo(t):
-            pick_bytes(x_offs, offs_l, False)
-            pick_words(x_offs, offs_l, False)
-        def s_xc(t):
-            late['cand'] = mx_tiles(O['cand_tag'])
-            pick_bytes(late['cand'], cand_l, True)
-            pick_words(late['cand'], cand_l, True)
-        def s_w1(t): quantize(round_weight(w1_raw, "w1", cp(O['w1']))[:], w1_q, whole)
-        def s_w3(t): quantize(round_weight(w3_raw, "w3", cp(O['w3']))[:], w3_q, whole)
-        def s_d(t):
-            acc = product(w2_q, x_two, t, O['dbanks'][t])
-            evac(O['dc'][t], d_win[t][:], acc[:])
-        def s_pa(t):
-            fetch(O['n3'][t], pa[t], d_win[t], n3_l, -1.0 if t in O['pe_u'] else 1.0)
-            if t not in O['pe_u']: tt('V', ka[t][:], pa[t][:], d_win[t][:], ALU.subtract)
-        def s_pb(t):
-            fetch(O['n4'][t], pb[t], d_win[t], n4_l, -1.0 if t in O['pe_u'] else 1.0)
-            if t not in O['pe_u']: tt('V', kb[t][:], pb[t][:], d_win[t][:], ALU.subtract)
-        def s_sq(t):
-            if t in O['pe_u']:
-                ua, ub = turn(d_win[t], pa[t]), turn(d_win[t], pb[t])
-                sq('S', ka[t][:], ua[:]); sq('S', kb[t][:], ub[:])
+        nc.vector.tensor_scalar(out=gs_neg[:], in0=gs_t[:], scalar1=-1.0, scalar2=None, op0=ALU.mult)
+
+        x_two, x_offs = mx_tiles("x_two"), mx_tiles("x_offs")
+        pick_words(x_two[0][:], two_l)
+        pick_bytes(x_two[1][:], two_l)
+        w2_q = quantize_weight(w2_raw, "w2", copy_on_scalar)
+        pick_bytes(x_offs[1][:], offs_l)
+        pick_words(x_offs[0][:], offs_l)
+        w1_q = quantize_weight(w1_raw, "w1", nc.vector.tensor_copy)
+
+        d, pa_neg, pb_neg = planes("d"), planes("pa_neg"), planes("pb_neg")
+        for t in PLANES:
+            copy_on_scalar(d[t][:], product(w2_q, x_two, t, DA_BANKS[t % 2])[:])
+            fetch_affine(t in VECTOR_N1_N3, pa_neg[t], d[t], n3_l, -1.0, 0.0)
+            fetch_affine(True, pb_neg[t], d[t], n4_l, -1.0, 0.0)
+
+        y_tanh, y_gate, st, kr, kr2 = planes("y_tanh"), planes("y_gate"), planes("st"), planes("kr"), planes("kr2")
+        st_joined = joined_planes("st_joined")
+        for t in PLANES:
+            y = product(w1_q, x_offs, t, Y_BANKS[t % 2])
+            nc.scalar.activation(out=y_tanh[t][:], in_=y[:], func=ACT.Tanh, scale=0.5)
+            fetch_affine(t in VECTOR_N1_N3, y_gate[t], y_tanh[t], n1_l, 0.5, 0.5)
+            scaled(st[t][:], y[:], gn_t[:, t : t + 1], ALU.mult, y_gate[t][:], ALU.mult)
+            nc.sync.dma_start(out=st_joined[:, t, :], in_=st[t][:])
+
+            differences = turn(d[t], pa_neg[t]), turn(d[t], pb_neg[t])
+            for weight, difference in zip((kr, kr2), differences):
+                nc.scalar.activation(out=weight[t][:], in_=difference[:], func=ACT.Square)
+            for weight in (kr, kr2):
+                nc.scalar.activation(out=weight[t][:], in_=turn(weight[t])[:], func=ACT.Exp, scale=-0.5)
+
+        w3_q = quantize_weight(w3_raw, "w3", nc.vector.tensor_copy)
+
+        st_far, den, num = joined_planes("st_far"), joined_planes("den"), joined_planes("num")
+        for t in PLANES:
+            fetch(False, st_far[:, t, :], st[t], n2_l)
+            scaled(den[:, t, :], kr[t][:], 0.5, ALU.add, kr2[t][:], ALU.add)
+            if t in VECTOR_DEN_SQUARE:
+                nc.vector.tensor_tensor(out=den[:, t, :], in0=den[:, t, :], in1=den[:, t, :], op=ALU.mult)
             else:
-                sq(O['sqa'][t], ka[t][:], ka[t][:]); sq(O['sqb'][t], kb[t][:], kb[t][:])
-        def s_ex(t):
-            for k in (ka, kb):
-                src = turn(k[t]) if (t in O['pe_u'] and O['mode'] == 'M') else k[t]
-                Sc.activation(out=k[t][:], in_=src[:], func=ACT.Exp, scale=-0.5)
-        def s_den(t):
-            if t in O['pe_u'] and O['mode'] == 'Y':
-                both = turn(ka[t], kb[t])
-                Sc.activation(out=den[:, t, :], in_=both[:], func=ACT.Square, bias=half_t[:])
-            else:
-                stt(den[:, t, :], ka[t][:], 0.5, kb[t][:], ALU.add, ALU.add)
-                sq(O['dsq'][t], den[:, t, :], den[:, t, :])
-        def s_pr(t):
-            for k, p_ in ((ka, pa), (kb, pb)):
-                back = turn(k[t], pool='vbanks') if (t in O['pe_u'] and O['mode'] == 'Y') else k[t]
-                stt(p_[t][:], back[:], (gs_neg if t in O['pe_u'] else gs_t)[:, t : t + 1], p_[t][:], ALU.mult, ALU.mult)
-            tt(O['num'][t], num[:, t, :], pa[t][:], pb[t][:])
-        def s_y(t):
-            y_acc[t] = product(w1_q, x_offs, t, O['ybanks'][t])
-            Sc.activation(out=th_win[t][:], in_=y_acc[t][:], func=ACT.Tanh, scale=0.5)
-        def s_st(t):
-            fetch(O['n1'][t], sg[t], th_win[t], n1_l, 0.5, 0.5)
-            stt(st_win[t][:], y_acc[t][:], gn_t[:, t : t + 1], sg[t][:], ALU.mult, ALU.mult)
-            nc.sync.dma_start(out=st4[:, t, :], in_=st_win[t][:])
-        def s_zf(t):
-            if O['n2'] == 'FFFF': fetch_fused(z_f[:, t, :], st_win[t], n2_l, st4[:, t, :], ALU.subtract)
-            else: fetch(O['n2'][t], z_f[:, t, :], st_win[t], n2_l)
-        def s_zq(t):
-            for h in range(O['zh']):
-                w = S // O['zh']
-                cols = slice(h * w, (h + 1) * w)
-                if O['n2'] == 'FFFF': V.tensor_scalar(out=z_bf[:, h * w * 4:(h + 1) * w * 4].rearrange("p (c i t) -> p c t i", i=4, t=PACK), in0=z_f[:, :, cols].rearrange("p t (c i) -> p c t i", i=4), scalar1=-1.0, scalar2=None, op0=ALU.mult)
-                else: V.tensor_tensor(out=z_bf[:, h * w * 4:(h + 1) * w * 4].rearrange("p (c i t) -> p c t i", i=4, t=PACK), in0=st4[:, :, cols].rearrange("p t (c i) -> p c t i", i=4), in1=z_f[:, :, cols].rearrange("p t (c i) -> p c t i", i=4), op=ALU.subtract)
-                quantize(z_bf[:, h * w * 4:(h + 1) * w * 4], z_q, cols)
-        def s_am(t):
-            a_acc[t] = product(w3_q, z_q, t, O['abanks'][t])
-            evac(O['ac'][t], a_win[t][:], a_acc[t][:], 0.5)
-            if O['n5'][t] == 'F': nc.sync.dma_start(out=a_twin[t][:], in_=a_win[t][:])
-        def s_as(t):
-            if O['n5'][t] == 'F': fetch_fused(a_sum[t], a_win[t], n5_l, a_twin[t], ALU.add)
-            else:
-                fetch(O['n5'][t], a_twin[t], a_win[t], n5_l)
-                tt('V', a_sum[t][:], a_win[t][:], a_twin[t][:])
-        def s_j(jb):
-            cols = slice(jb * P, (jb + 1) * P)
-            rec = keep.tile([P, PACK, P], F32, name=f"rec{jb}")
-            nc.scalar.activation(out=rec[:], in_=den[:, :, cols], func=ACT.Abs_reciprocal_sqrt)
-            z2_bf = keep.tile([P, P * PACK], BF16, name=f"z2_bf{jb}", align_bytes=64)
-            nc.vector.tensor_tensor(
-                out=z2_bf[:].rearrange("p (c i t) -> p c t i", i=4, t=PACK),
-                in0=num[:, :, cols].rearrange("p t (c i) -> p c t i", i=4),
-                in1=rec[:].rearrange("p t (c i) -> p c t i", i=4),
-                op=ALU.mult,
-            )
+                nc.scalar.activation(out=den[:, t, :], in_=den[:, t, :], func=ACT.Square)
+            for weight, value in ((kr, pa_neg), (kr2, pb_neg)):
+                scaled(value[t][:], weight[t][:], gs_neg[:, t : t + 1], ALU.mult, value[t][:], ALU.mult)
+            nc.vector.tensor_tensor(out=num[:, t, :], in0=pa_neg[t][:], in1=pb_neg[t][:], op=ALU.add)
+
+        z_q = mx_tiles("z")
+        z_bf = keep.tile([P, S * PACK], BF16, name="z_bf", align_bytes=64)
+        for h in range(2):
+            cols = slice(h * HALF, (h + 1) * HALF)
+            values = z_bf[:, PACK * cols.start : PACK * cols.stop]
+            interleave(values, st_joined[:, :, cols], st_far[:, :, cols], ALU.subtract)
+            quantize(values, z_q, cols)
+
+        x_cand = mx_tiles("x_offs")
+        pick_bytes(x_cand[1][:].rearrange("p (t m) -> p m t", t=PACK), cand_l)
+        pick_words(x_cand[0][:].rearrange("p (t m) -> p m t", t=PACK), cand_l)
+
+        z2_q = mx_tiles("z2")
+        for block in range(S // P):
+            cols = slice(block * P, (block + 1) * P)
+            inverse = keep.tile([P, PACK, P], F32, name=f"inverse{block}")
+            nc.scalar.activation(out=inverse[:], in_=den[:, :, cols], func=ACT.Abs_reciprocal_sqrt)
+            z2_bf = keep.tile([P, P * PACK], BF16, name=f"z2_bf{block}", align_bytes=64)
+            interleave(z2_bf[:], num[:, :, cols], inverse[:], ALU.mult)
             quantize(z2_bf[:], z2_q, cols)
-        def s_bm(t):
-            b_acc[t] = product(late['cand'], z2_q, t, O['bbanks'][t])
-            evac(O['bc'][t], b_win[t][:], b_acc[t][:])
-        def s_g(t):
-            fetch(O['n6'][t], gate[t], b_win[t], n6_l)
-            tt('V', gate[t][:], gate[t][:], b_acc[t][:])
-            nc.scalar.activation(out=gate[t][:], in_=gate[t][:], func=ACT.Tanh, scale=0.03125)
-        def s_o(t):
-            stt(gate[t][:], gate[t][:], 1.0, a_sum[t][:], ALU.add, ALU.mult)
-            nc.sync.dma_start(out=out_rows[t], in_=gate[t][:])
-        L = dict(w1=s_w1, w2=s_w2, w3=s_w3, xt=s_xt, xo=s_xo, xc=s_xc, d=s_d, pa=s_pa, pb=s_pb, sq=s_sq, ex=s_ex, den=s_den, pr=s_pr, y=s_y, st=s_st, zf=s_zf, zq=s_zq, am=s_am, j=s_j, bm=s_bm, g=s_g, o=s_o)
-        L['as'] = s_as
-        for name, t in O['order']:
-            L[name](t)
+
+        a_half, a_other, a_sum = planes("a_half"), planes("a_other"), planes("a_sum")
+        for t in PLANES:
+            copy_on_scalar(a_half[t][:], product(w3_q, z_q, t, DA_BANKS[t % 2])[:], scale=0.5)
+            if t not in SCALAR_N5:
+                nc.sync.dma_start(out=a_other[t][:], in_=a_half[t][:])
+        b, gate = planes("b"), planes("gate")
+        for t in PLANES:
+            acc = product(x_cand, z2_q, t, B_BANKS[t])
+            if t in VECTOR_B_COPY:
+                nc.vector.tensor_copy(out=b[t][:], in_=acc[:])
+            else:
+                copy_on_scalar(b[t][:], acc[:])
+
+        for t in PLANES:
+            fetch(t in VECTOR_N6, gate[t], b[t], n6_l)
+            nc.scalar.activation(out=gate[t][:], in_=turn(b[t], gate[t])[:], func=ACT.Tanh, scale=0.0625 / 2)
+
+        out_planes = out.rearrange("(p t) n -> t p n", t=PACK)
+        for t in PLANES:
+            if t in SCALAR_N5:
+                fetch(False, a_other[t], a_half[t], n5_l)
+                nc.vector.tensor_tensor(out=a_sum[t][:], in0=a_half[t][:], in1=a_other[t][:], op=ALU.add)
+            else:
+                for cols, list_cols in HALVES:
+                    nc.vector.tensor_tensor(
+                        out=a_sum[t][:, cols],
+                        in0=a_half[t][:].indirect(n5_l[:, list_cols]),
+                        in1=a_other[t][:, cols],
+                        op=ALU.add,
+                    )
+            scaled(gate[t][:], turn(gate[t])[:], 1.0, ALU.add, a_sum[t][:], ALU.mult)
+            nc.sync.dma_start(out=out_planes[t], in_=gate[t][:])

@@ -28,10 +28,9 @@ HALVES = [(slice(h * HALF, (h + 1) * HALF), slice(h * HALF // LIST_ROWS, (h + 1)
 
 DA_BANKS, Y_BANKS, B_BANKS, TURN_BANKS = (0, 1), (2, 3), (2, 3, 0, 1), (4, 5, 6, 7)
 
-VECTOR_N1_N3 = (3,)
-VECTOR_N6 = (1, 3)
+VECTOR_N2_N3 = (3,)
+VECTOR_N1_N6 = (1, 3)
 VECTOR_B_COPY = (0, 1)
-VECTOR_DEN_SQUARE = (0,)
 SCALAR_N5 = (0,)
 
 
@@ -185,6 +184,8 @@ def tile_picked_tfcdtriebhopgkern_none_p_kernel(
 
         identity = keep.tile([P, P], F32, name="identity")
         make_identity(nc, identity[:])
+        half = keep.tile([P, 1], F32, name="half")
+        nc.vector.memset(half[:], 0.5)
         gs_neg = keep.tile([P, PACK], F32, name="gs_neg")
         nc.vector.tensor_scalar(out=gs_neg[:], in0=gs_t[:], scalar1=-1.0, scalar2=None, op0=ALU.mult)
 
@@ -199,7 +200,7 @@ def tile_picked_tfcdtriebhopgkern_none_p_kernel(
         d, pa_neg, pb_neg = planes("d"), planes("pa_neg"), planes("pb_neg")
         for t in PLANES:
             copy_on_scalar(d[t][:], product(w2_q, x_two, t, DA_BANKS[t % 2])[:])
-            fetch_affine(t in VECTOR_N1_N3, pa_neg[t], d[t], n3_l, -1.0, 0.0)
+            fetch_affine(t in VECTOR_N2_N3, pa_neg[t], d[t], n3_l, -1.0, 0.0)
             fetch_affine(True, pb_neg[t], d[t], n4_l, -1.0, 0.0)
 
         y_tanh, y_gate, st, kr, kr2 = planes("y_tanh"), planes("y_gate"), planes("st"), planes("kr"), planes("kr2")
@@ -207,7 +208,7 @@ def tile_picked_tfcdtriebhopgkern_none_p_kernel(
         for t in PLANES:
             y = product(w1_q, x_offs, t, Y_BANKS[t % 2])
             nc.scalar.activation(out=y_tanh[t][:], in_=y[:], func=ACT.Tanh, scale=0.5)
-            fetch_affine(t in VECTOR_N1_N3, y_gate[t], y_tanh[t], n1_l, 0.5, 0.5)
+            fetch_affine(t in VECTOR_N1_N6, y_gate[t], y_tanh[t], n1_l, 0.5, 0.5)
             scaled(st[t][:], y[:], gn_t[:, t : t + 1], ALU.mult, y_gate[t][:], ALU.mult)
             nc.sync.dma_start(out=st_joined[:, t, :], in_=st[t][:])
 
@@ -219,14 +220,16 @@ def tile_picked_tfcdtriebhopgkern_none_p_kernel(
 
         w3_q = quantize_weight(w3_raw, "w3", nc.vector.tensor_copy)
 
-        st_far, den, num = joined_planes("st_far"), joined_planes("den"), joined_planes("num")
+        st_far, num = joined_planes("st_far"), joined_planes("num")
+        den_square = keep.tile([P, S // P, PACK, P], F32, name="den_square")
         for t in PLANES:
-            fetch(False, st_far[:, t, :], st[t], n2_l)
-            scaled(den[:, t, :], kr[t][:], 0.5, ALU.add, kr2[t][:], ALU.add)
-            if t in VECTOR_DEN_SQUARE:
-                nc.vector.tensor_tensor(out=den[:, t, :], in0=den[:, t, :], in1=den[:, t, :], op=ALU.mult)
-            else:
-                nc.scalar.activation(out=den[:, t, :], in_=den[:, t, :], func=ACT.Square)
+            fetch(t in VECTOR_N2_N3, st_far[:, t, :], st[t], n2_l)
+            nc.scalar.activation(
+                out=den_square[:, :, t, :],
+                in_=turn(kr[t], kr2[t])[:].rearrange("j (block p) -> j block p", p=P),
+                func=ACT.Square,
+                bias=half[:],
+            )
             for weight, value in ((kr, pa_neg), (kr2, pb_neg)):
                 scaled(value[t][:], weight[t][:], gs_neg[:, t : t + 1], ALU.mult, value[t][:], ALU.mult)
             nc.vector.tensor_tensor(out=num[:, t, :], in0=pa_neg[t][:], in1=pb_neg[t][:], op=ALU.add)
@@ -247,7 +250,12 @@ def tile_picked_tfcdtriebhopgkern_none_p_kernel(
         for block in range(S // P):
             cols = slice(block * P, (block + 1) * P)
             inverse = keep.tile([P, PACK, P], F32, name=f"inverse{block}")
-            nc.scalar.activation(out=inverse[:], in_=den[:, :, cols], func=ACT.Abs_reciprocal_sqrt)
+            back = psum.tile([P, PACK, P], F32, name="back", tag=f"bank{TURN_BANKS[block]}")
+            for t in PLANES:
+                nc.tensor.matmul(
+                    out=back[:, t, :], lhsT=den_square[:, block, t, :], rhs=identity[:], start=True, stop=True, is_transpose=True
+                )
+            nc.scalar.activation(out=inverse[:], in_=back[:], func=ACT.Abs_reciprocal_sqrt)
             z2_bf = keep.tile([P, P * PACK], BF16, name=f"z2_bf{block}", align_bytes=64)
             interleave(z2_bf[:], num[:, :, cols], inverse[:], ALU.mult)
             quantize(z2_bf[:], z2_q, cols)
@@ -266,7 +274,7 @@ def tile_picked_tfcdtriebhopgkern_none_p_kernel(
                 copy_on_scalar(b[t][:], acc[:])
 
         for t in PLANES:
-            fetch(t in VECTOR_N6, gate[t], b[t], n6_l)
+            fetch(t in VECTOR_N1_N6, gate[t], b[t], n6_l)
             nc.scalar.activation(out=gate[t][:], in_=turn(b[t], gate[t])[:], func=ACT.Tanh, scale=0.0625 / 2)
 
         out_planes = out.rearrange("(p t) n -> t p n", t=PACK)

from contextlib import ExitStack

import concourse.mybir as mybir
from concourse.masks import make_identity

T, S = 2048, 512
FLOPS = 4 * 2 * 512 * 512 * 512

F32 = mybir.dt.float32
BF16 = mybir.dt.bfloat16
I32 = mybir.dt.int32
U32 = mybir.dt.uint32
U16 = mybir.dt.uint16
U8 = mybir.dt.uint8
FP8X4 = mybir.dt.float8_e4m3fn_x4
ACT = mybir.ActivationFunctionType
ALU = mybir.AluOpType

P = 128
PACK = 4
PLANES = range(PACK)
QUADRANT = 32
LIST_ROWS = 16
LINE = 4
ALL = slice(0, S)
HALF = S // 2
HALVES = [(slice(h * HALF, (h + 1) * HALF), slice(h * HALF // LIST_ROWS, (h + 1) * HALF // LIST_ROWS)) for h in range(2)]

DA_BANKS, Y_BANKS, B_BANKS, TURN_BANKS = (0, 1), (2, 3), (2, 3, 0, 1), (4, 5, 6, 7)

VECTOR_N2_N3 = (3,)
VECTOR_N1_N6 = (1, 3)
VECTOR_B_COPY = (0, 1)
SCALAR_N5 = (0,)


def tile_picked_tfcdtriebhopgkern_none_p_kernel(
    tc, x_words, x_scales, w1, w2, gn, w3, gs, offs, two, n1, n2, n3, n4, cand, n5, n6, out
):
    nc = tc.nc
    with ExitStack() as ctx:
        keep = ctx.enter_context(tc.tile_pool(name="keep", bufs=1))
        psum = ctx.enter_context(tc.psum_pool(name="psum", bufs=1))

        def planes(name):
            return [keep.tile([P, S], F32, name=f"{name}{t}") for t in PLANES]

        def joined_planes(name):
            return keep.tile([P, PACK, S], F32, name=name)

        def load_list(src, name):
            tile = keep.tile([P, S // LIST_ROWS], U16, name=name)
            nc.sync.dma_start(tile[:], src)
            return tile

        def load_weight(w, name, pieces):
            rows = w.rearrange("(p j) c -> p j c", j=PACK)
            step = PACK // pieces
            raws = []
            for h in range(pieces):
                raw = keep.tile([P, step, S], F32, name=f"{name}_raw{h}")
                nc.sync.dma_start(out=raw[:], in_=rows[:, h * step : (h + 1) * step, :])
                raws.append(raw)
            return raws

        def load_gain(g, name):
            tile = keep.tile([P, PACK], F32, name=name)
            nc.sync.dma_start(out=tile[:], in_=g.rearrange("(p t) o -> p (t o)", t=PACK))
            return tile

        def mx_tiles(name):
            words = keep.tile([P, S], U32, name=f"{name}_words", align_bytes=64)
            scales = keep.tile([P, S], U8, name=f"{name}_scales", align_bytes=64)
            return words, scales

        def quantize(values, operand, cols):
            words, scales = operand
            nc.vector.quantize_mx(out=words[:, cols].bitcast(FP8X4), scales=scales[:, cols], in_=values)

        def copy_on_scalar(out, in_, scale=1.0):
            nc.scalar.activation(out=out, in_=in_, func=ACT.Copy, scale=scale)

        def quantize_weight(raws, name, copy):
            grouped = keep.tile([P, PACK * S], BF16, name=f"{name}_bf", align_bytes=64)
            dealt = grouped[:].rearrange("p (t m j) -> p m j t", t=PACK, j=PACK)
            step = PACK // len(raws)
            for h, raw in enumerate(raws):
                copy(out=dealt[:, :, h * step : (h + 1) * step, :], in_=raw[:].rearrange("p j (m t) -> p m j t", t=PACK))
            operand = mx_tiles(name)
            quantize(grouped[:], operand, ALL)
            return operand

        def product(stationary, moving, t, bank):
            acc = psum.tile([P, S], F32, name="acc", tag=f"bank{bank}")
            cols = slice(t * P, (t + 1) * P)
            nc.tensor.matmul_mx(
                out=acc[:],
                lhsT=stationary[0][:, cols].bitcast(FP8X4),
                lhsT_scale=stationary[1][:, cols],
                rhs=moving[0][:].bitcast(FP8X4),
                rhs_scale=moving[1][:],
                start=True,
                stop=True,
            )
            return acc

        turns = []

        def turn(*tiles):
            turns.append(tiles)
            acc = psum.tile([P, S], F32, name="turned", tag=f"bank{TURN_BANKS[len(turns) % len(TURN_BANKS)]}")
            for block in range(S // P):
                cols = slice(block * P, (block + 1) * P)
                for n, tile in enumerate(tiles):
                    nc.tensor.matmul(
                        out=acc[:, cols],
                        lhsT=tile[:, cols],
                        rhs=identity[:],
                        start=n == 0,
                        stop=n == len(tiles) - 1,
                        is_transpose=True,
                    )
            return acc

        def fetch(on_vector, dst, window, places):
            for cols, list_cols in HALVES:
                picked = window[:].indirect(places[:, list_cols])
                if on_vector:
                    nc.vector.tensor_copy(out=dst[:, cols], in_=picked)
                else:
                    nc.scalar.activation(out=dst[:, cols], in_=picked, func=ACT.Copy)

        def fetch_affine(on_vector, dst, window, places, scale, bias):
            for cols, list_cols in HALVES:
                picked = window[:].indirect(places[:, list_cols])
                if on_vector:
                    nc.vector.tensor_scalar(
                        out=dst[:, cols], in0=picked, scalar1=scale, scalar2=bias, op0=ALU.mult, op1=ALU.add
                    )
                else:
                    nc.scalar.activation(out=dst[:, cols], in_=picked, func=ACT.Copy, scale=scale, bias=bias)

        def interleave(dst, in0, in1, op):
            nc.vector.tensor_tensor(
                out=dst.rearrange("p (c i t) -> p c t i", i=LINE, t=PACK),
                in0=in0.rearrange("p t (c i) -> p c t i", i=LINE),
                in1=in1.rearrange("p t (c i) -> p c t i", i=LINE),
                op=op,
            )

        def scaled(dst, in0, scalar, op0, in1, op1):
            nc.vector.scalar_tensor_tensor(out=dst, in0=in0, scalar=scalar, in1=in1, op0=op0, op1=op1)

        x_bytes = keep.tile([P, T], U8, name="x_bytes")
        nc.vector.memset(x_bytes[:].bitcast(I32), 0)
        x_rows = keep.tile([P, T // 4], I32, name="x_rows")
        scale_rows = [slice(QUADRANT * q, QUADRANT * q + 4) for q in range(P // QUADRANT)]
        for q, rows in enumerate(scale_rows):
            nc.sync.dma_start(out=x_rows[rows, :], in_=x_scales[0, 4 * q : 4 * q + 4, :].bitcast(I32))
        two_l = load_list(two, "two")
        offs_l = load_list(offs, "offs")
        w2_raw = load_weight(w2, "w2", pieces=2)
        x_table = keep.tile([P, T], I32, name="x_table")
        nc.sync.dma_start(out=x_table[:], in_=x_words[0].rearrange("p n t -> p (n t)").bitcast(I32))
        n3_l = load_list(n3, "n3")
        n4_l = load_list(n4, "n4")
        w1_raw = load_weight(w1, "w1", pieces=1)
        gs_t = load_gain(gs, "gs")
        gn_t = load_gain(gn, "gn")
        n1_l = load_list(n1, "n1")
        n2_l = load_list(n2, "n2")
        cand_l = load_list(cand, "cand")
        w3_raw = load_weight(w3, "w3", pieces=1)
        n5_l = load_list(n5, "n5")
        n6_l = load_list(n6, "n6")
        for rows in scale_rows:
            nc.vector.tensor_copy(out=x_bytes[rows, :].bitcast(I32), in_=x_rows[rows, :])

        def pick_words(dst, places):
            nc.vector.tensor_copy(out=dst, in_=x_table[:].bitcast(U32).indirect(places[:]))

        def pick_bytes(dst, places):
            nc.vector.tensor_copy(out=dst, in_=x_bytes[:].indirect(places[:]))

        identity = keep.tile([P, P], F32, name="identity")
        make_identity(nc, identity[:])
        half = keep.tile([P, 1], F32, name="half")
        nc.vector.memset(half[:], 0.5)
        gs_neg = keep.tile([P, PACK], F32, name="gs_neg")
        nc.vector.tensor_scalar(out=gs_neg[:], in0=gs_t[:], scalar1=-1.0, scalar2=None, op0=ALU.mult)

        x_two, x_offs = mx_tiles("x_two"), mx_tiles("x_offs")
        pick_words(x_two[0][:], two_l)
        pick_bytes(x_two[1][:], two_l)
        w2_q = quantize_weight(w2_raw, "w2", copy_on_scalar)
        pick_bytes(x_offs[1][:], offs_l)
        pick_words(x_offs[0][:], offs_l)
        w1_q = quantize_weight(w1_raw, "w1", nc.vector.tensor_copy)

        d, pa_neg, pb_neg = planes("d"), planes("pa_neg"), planes("pb_neg")
        for t in PLANES:
            copy_on_scalar(d[t][:], product(w2_q, x_two, t, DA_BANKS[t % 2])[:])
            fetch_affine(t in VECTOR_N2_N3, pa_neg[t], d[t], n3_l, -1.0, 0.0)
            fetch_affine(True, pb_neg[t], d[t], n4_l, -1.0, 0.0)

        y_tanh, y_gate, st, kr, kr2 = planes("y_tanh"), planes("y_gate"), planes("st"), planes("kr"), planes("kr2")
        st_joined = joined_planes("st_joined")
        for t in PLANES:
            y = product(w1_q, x_offs, t, Y_BANKS[t % 2])
            nc.scalar.activation(out=y_tanh[t][:], in_=y[:], func=ACT.Tanh, scale=0.5)
            fetch_affine(t in VECTOR_N1_N6, y_gate[t], y_tanh[t], n1_l, 0.5, 0.5)
            scaled(st[t][:], y[:], gn_t[:, t : t + 1], ALU.mult, y_gate[t][:], ALU.mult)
            nc.sync.dma_start(out=st_joined[:, t, :], in_=st[t][:])

            differences = turn(d[t], pa_neg[t]), turn(d[t], pb_neg[t])
            for weight, difference in zip((kr, kr2), differences):
                nc.scalar.activation(out=weight[t][:], in_=difference[:], func=ACT.Square)
            for weight in (kr, kr2):
                nc.scalar.activation(out=weight[t][:], in_=turn(weight[t])[:], func=ACT.Exp, scale=-0.5)

        w3_q = quantize_weight(w3_raw, "w3", nc.vector.tensor_copy)

        st_far, num = joined_planes("st_far"), joined_planes("num")
        den_square = keep.tile([P, S // P, PACK, P], F32, name="den_square")
        for t in PLANES:
            fetch(t in VECTOR_N2_N3, st_far[:, t, :], st[t], n2_l)
            nc.scalar.activation(
                out=den_square[:, :, t, :],
                in_=turn(kr[t], kr2[t])[:].rearrange("j (block p) -> j block p", p=P),
                func=ACT.Square,
                bias=half[:],
            )
            for weight, value in ((kr, pa_neg), (kr2, pb_neg)):
                scaled(value[t][:], weight[t][:], gs_neg[:, t : t + 1], ALU.mult, value[t][:], ALU.mult)
            nc.vector.tensor_tensor(out=num[:, t, :], in0=pa_neg[t][:], in1=pb_neg[t][:], op=ALU.add)

        z_q = mx_tiles("z")
        z_bf = keep.tile([P, S * PACK], BF16, name="z_bf", align_bytes=64)
        for h in range(2):
            cols = slice(h * HALF, (h + 1) * HALF)
            values = z_bf[:, PACK * cols.start : PACK * cols.stop]
            interleave(values, st_joined[:, :, cols], st_far[:, :, cols], ALU.subtract)
            quantize(values, z_q, cols)

        x_cand = mx_tiles("x_offs")
        pick_bytes(x_cand[1][:].rearrange("p (t m) -> p m t", t=PACK), cand_l)
        pick_words(x_cand[0][:].rearrange("p (t m) -> p m t", t=PACK), cand_l)

        z2_q = mx_tiles("z2")
        for block in range(S // P):
            cols = slice(block * P, (block + 1) * P)
            inverse = keep.tile([P, PACK, P], F32, name=f"inverse{block}")
            back = psum.tile([P, PACK, P], F32, name="back", tag=f"bank{TURN_BANKS[block]}")
            for t in PLANES:
                nc.tensor.matmul(
                    out=back[:, t, :], lhsT=den_square[:, block, t, :], rhs=identity[:], start=True, stop=True, is_transpose=True
                )
            nc.scalar.activation(out=inverse[:], in_=back[:], func=ACT.Abs_reciprocal_sqrt)
            z2_bf = keep.tile([P, P * PACK], BF16, name=f"z2_bf{block}", align_bytes=64)
            interleave(z2_bf[:], num[:, :, cols], inverse[:], ALU.mult)
            quantize(z2_bf[:], z2_q, cols)

        a_half, a_other, a_sum = planes("a_half"), planes("a_other"), planes("a_sum")
        for t in PLANES:
            copy_on_scalar(a_half[t][:], product(w3_q, z_q, t, DA_BANKS[t % 2])[:], scale=0.5)
            if t not in SCALAR_N5:
                nc.sync.dma_start(out=a_other[t][:], in_=a_half[t][:])
        b, gate = planes("b"), planes("gate")
        for t in PLANES:
            acc = product(x_cand, z2_q, t, B_BANKS[t])
            if t in VECTOR_B_COPY:
                nc.vector.tensor_copy(out=b[t][:], in_=acc[:])
            else:
                copy_on_scalar(b[t][:], acc[:])

        for t in PLANES:
            fetch(t in VECTOR_N1_N6, gate[t], b[t], n6_l)
            nc.scalar.activation(out=gate[t][:], in_=turn(b[t], gate[t])[:], func=ACT.Tanh, scale=0.0625 / 2)

        out_planes = out.rearrange("(p t) n -> t p n", t=PACK)
        for t in PLANES:
            if t in SCALAR_N5:
                fetch(False, a_other[t], a_half[t], n5_l)
                nc.vector.tensor_tensor(out=a_sum[t][:], in0=a_half[t][:], in1=a_other[t][:], op=ALU.add)
            else:
                for cols, list_cols in HALVES:
                    nc.vector.tensor_tensor(
                        out=a_sum[t][:, cols],
                        in0=a_half[t][:].indirect(n5_l[:, list_cols]),
                        in1=a_other[t][:, cols],
                        op=ALU.add,
                    )
            scaled(gate[t][:], turn(gate[t])[:], 1.0, ALU.add, a_sum[t][:], ALU.mult)
            nc.sync.dma_start(out=out_planes[t], in_=gate[t][:])
